import numpy as np
CORES = [211,219,227,235,243,251,83,91,99,107,115,123]
N = 12
F = 128
BOUND = 22152.5
def setup_inputs(rng):
    gr = rng.standard_normal((1, 128, N * F), dtype=np.float32) + rng.standard_normal((N, 128, N * F), dtype=np.float32)
    return {"gr": gr}
def setup_inputs_big(rng):
    d = setup_inputs(rng)
    for k in ("gr",): d[k] = (d[k].astype(np.float32) * 1024.0).astype(d[k].dtype)
    return d
def setup_inputs_small(rng):
    d = setup_inputs(rng)
    for k in ("gr",): d[k] = (d[k].astype(np.float32) * (1 / 1024.0)).astype(d[k].dtype)
    return d
def setup_inputs_apart(rng):
    d = setup_inputs(rng)
    f = (10.0 ** rng.permutation(np.linspace(-1.5, 1.5, N))).astype(np.float32).reshape(N, 1, 1)
    for k in ("gr",): d[k] = (d[k].astype(np.float32) * f).astype(d[k].dtype)
    return d
def setup_inputs_far(rng):
    d = setup_inputs(rng)
    for k in ("gr",): d[k] = (d[k].astype(np.float32) * 16384.0).astype(d[k].dtype)
    return d
def setup_inputs_over(rng):
    d = setup_inputs(rng)
    f = np.float32(10.0 ** rng.uniform(1.5, 3.5)) * np.where(rng.random((1, 128, N * F)) < 0.5, 0.1, 1.0).astype(np.float32)
    for k in ("gr",): d[k] = (d[k].astype(np.float32) * f).astype(d[k].dtype)
    return d
def reference(gr):
    s = gr.astype(np.float64).sum(axis=0)
    nrm = np.sqrt((s ** 2).sum())
    s = s * min(1.0, BOUND / nrm)
    return {"y": np.stack([s[:, F * r:F * r + F] for r in range(N)]).astype(np.float32)}

@@ -1,0 +1,137 @@
+from concourse.bass import DstId, RemoteDMATransfer
+from concourse.mybir import AluOpType, AxisListType, ActivationFunctionType
+
+F = 128
+SCRATCH = {
+    "x": ("sbuf", [128, 12 * F], "float32"),
+    "lm": ("sbuf", [128, 6 * F], "float32"),
+    "lp": ("sbuf", [128, 5 * F], "float32"),
+    "sq": ("sbuf", [128, F], "float32"),
+    "yb": ("sbuf", [128, F], "float32"),
+    "qs": ("sbuf", [128, F], "float32"),
+    "ones": ("sbuf", [128, F], "float32"),
+    "sc": ("sbuf", [128, 12], "float32"),
+    "qall": ("dram", [12, 128, 1], "float32"),
+    "acc": ("psum", [128, 512], "float32"),
+    "tot": ("psum", [128, 512], "float32"),
+}
+SEMAPHORES = ["ld0", "ld1", "ld2", "ld3", "ld4", "ld5", "ma0", "ma1", "ma2", "pa0", "pa1", "pa2",
+              "sent", "vs", "as1", "qo", "qa", "qg", "cst", "ps", "st"]
+
+
+def _split(mask, n):
+    eng = [b for b in range(16) if (mask >> b) & 1]
+    per = len(eng) // n
+    return [sum(1 << e for e in eng[j * per:(j + 1) * per]) for j in range(n)]
+
+
+def rank_program(g, core, T, topo):
+    me = T.rank_of(core)
+    if me is None:
+        return
+    S = T.sem
+    cores = list(T.cores)
+    bound = float(T.tables["BOUND"])
+    mate = [c for c in cores if topo.mates(core, c)][0]
+    plane = [c for c in cores if c == core or topo.same_plane(core, c)]
+    mplane = [c for c in cores if c == mate or topo.same_plane(mate, c)]
+    k, km, P = plane.index(core), mplane.index(mate), len(plane)
+    peer = [plane[(k + d) % P] for d in range(1, P)]
+    mpeer = [mplane[(km + d) % P] for d in range(1, P)]
+    order = [T.rank_of(c) for c in mpeer + [mate] + peer + [core]]
+
+    def sl(t, s, n=1):
+        return t[:, s * F:(s + n) * F]
+
+    def dst(c):
+        rid, pid = topo.addr(c, core)
+        return DstId(rid=rid, pnc=pid)
+
+    v, a, sy, pe = g.vector, g.scalar, g.sync, g.tensor
+    ld = [S.ld0, S.ld1, S.ld2, S.ld3, S.ld4, S.ld5]
+    ma = [S.ma0, S.ma1, S.ma2]
+    pa = [S.pa0, S.pa1, S.pa2]
+
+    for s, b in enumerate(order):
+        q = sy if s % 2 == 0 else a
+        q.dma_start(sl(T.x, s), T.gr[:, b * F:(b + 1) * F]).then_inc(ld[s // 2], 16)
+    v.memset(T.ones[0:12, :], 1.0).then_inc(S.cst, 1)
+
+    mm = topo.mask(core, mate)
+    ne = len(_split(mm, 1)) and sum((mm >> b) & 1 for b in range(16))
+    rid, pid = topo.addr(mate, core)
+    sent = 0
+    for p in range(3):
+        g.wait_ge(ld[p], 32)
+        g.remote_dma(out_ap=sl(T.lm, 2 * p, 2), in_ap=sl(T.x, 2 * p, 2), remote_sem=ma[p], local_sem=S.sent,
+                     pid=pid, routing_id=rid, dma_engine_mask=mm)
+        sent += ne
+
+    batches = [[0, 1], [2, 3], [4]]
+    for p, ds in enumerate(batches):
+        g.wait_ge(ld[3 + p], 32)
+        g.wait_ge(ma[p], ne)
+        masks = _split(topo.mask(core, peer[ds[0]]), len(ds))
+        trs = []
+        for d, m in zip(ds, masks):
+            trs.append(RemoteDMATransfer(dst_ids=[dst(peer[d])], dma_engine_mask=m, remote_sem=pa[p],
+                                         srcs=[sl(T.x, 6 + d), sl(T.lm, d)], dsts=[sl(T.lp, d)], alu_op=1))
+            sent += sum((m >> b) & 1 for b in range(16))
+        g.remote_dma_fused(trs, local_sem=S.sent)
+
+    acc = T.acc[:, 0:F]
+    v.wait_ge(ld[5], 32)
+    v.wait_ge(ma[2], ne)
+    v.tensor_tensor(acc, sl(T.x, 11), sl(T.lm, 5), AluOpType.add).then_inc(S.vs, 1)
+    n = 1
+    for p, ds in enumerate(batches):
+        v.wait_ge(pa[p], ne)
+        for d in ds:
+            v.wait_ge(S.vs, n)
+            v.tensor_tensor(acc, acc, sl(T.lp, d), AluOpType.add).then_inc(S.vs, 1)
+            n += 1
+
+    a.wait_ge(S.vs, n)
+    a.activation(T.sq[:], acc, ActivationFunctionType.Square, accum_out=T.sc[:, 0:1]).then_inc(S.as1, 1)
+    a.wait_ge(S.as1, 1)
+    a.dma_start(T.qall[me], T.sc[:, 0:1]).then_inc(S.qo, 16)
+
+    others = [c for c in cores if c != core]
+    common = topo.mask(core, others[0])
+    for c in others:
+        common &= topo.mask(core, c)
+    ones_m = _split(common, sum((common >> b) & 1 for b in range(16)))
+    groups = [others[j::len(ones_m)] for j in range(len(ones_m))]
+    trs = []
+    for m, grp in zip(ones_m, groups):
+        if grp:
+            trs.append(RemoteDMATransfer(dst_ids=[dst(c) for c in grp], dma_engine_mask=m, remote_sem=S.qa,
+                                         srcs=[T.qall[me]], dsts=[T.qall[me] for c in grp], alu_op=0))
+            sent += 1
+    g.wait_ge(S.qo, 16)
+    g.remote_dma_fused(trs, local_sem=S.sent)
+    g.wait_ge(S.sent, sent)
+
+    sy.wait_ge(S.qo, 16)
+    sy.wait_ge(S.qa, len(others))
+    sy.dma_start(T.qs[0:12, :], T.qall[:]).then_inc(S.qg, 16)
+
+    v.wait_ge(S.qg, 16)
+    v.tensor_reduce(T.sc[0:12, 4:5], T.qs[0:12, :], AxisListType.X, AluOpType.add).then_inc(S.vs, 1)
+    n += 1
+    pe.wait_ge(S.cst, 1)
+    pe.wait_ge(S.vs, n)
+    pe.matmul(T.tot[:, 0:1], T.ones[0:12, :], T.sc[0:12, 4:5], True, True).then_inc(S.ps, 1)
+    v.wait_ge(S.ps, 1)
+    v.tensor_scalar(T.sc[:, 8:9], T.tot[:, 0:1], 1.0 / (bound * bound), 1.0, AluOpType.mult, AluOpType.max).then_inc(S.vs, 1)
+    n += 1
+    v.wait_ge(S.vs, n)
+    v.reciprocal(T.sc[:, 9:10], T.sc[:, 8:9]).then_inc(S.vs, 1)
+    n += 1
+    a.wait_ge(S.vs, n)
+    a.activation(T.sc[:, 10:11], T.sc[:, 9:10], ActivationFunctionType.Sqrt).then_inc(S.as1, 1)
+    a.wait_ge(S.as1, 2)
+    a.activation(T.yb[:], acc, ActivationFunctionType.Copy, scale=T.sc[:, 10:11]).then_inc(S.as1, 1)
+    a.wait_ge(S.as1, 3)
+    a.dma_start(T.y[:], T.yb[:]).then_inc(S.st, 16)
+    a.wait_ge(S.st, 16)

@@ -2,21 +2,30 @@ from concourse.bass import DstId, RemoteDMATransfer
 from concourse.mybir import AluOpType, AxisListType, ActivationFunctionType
 
 F = 128
+QP, QC = 32, 48
 SCRATCH = {
-    "x": ("sbuf", [128, 12 * F], "float32"),
-    "lm": ("sbuf", [128, 6 * F], "float32"),
+    "xd": ("dram", [5, 128, F], "float32"),
+    "lmd": ("dram", [5, 128, F], "float32"),
+    "x": ("sbuf", [128, 7 * F], "float32"),
+    "lm": ("sbuf", [128, F], "float32"),
     "lp": ("sbuf", [128, 5 * F], "float32"),
     "sq": ("sbuf", [128, F], "float32"),
     "yb": ("sbuf", [128, F], "float32"),
-    "qs": ("sbuf", [128, F], "float32"),
-    "ones": ("sbuf", [128, F], "float32"),
+    "qs": ("sbuf", [128, QC], "float32"),
+    "w": ("sbuf", [128, F], "float32"),
+    "cl": ("sbuf", [128, QC], "float32"),
+    "sn": ("sbuf", [128, QC], "float32"),
     "sc": ("sbuf", [128, 12], "float32"),
     "qall": ("dram", [12, 128, 1], "float32"),
     "acc": ("psum", [128, 512], "float32"),
     "tot": ("psum", [128, 512], "float32"),
 }
-SEMAPHORES = ["ld0", "ld1", "ld2", "ld3", "ld4", "ld5", "ma0", "ma1", "ma2", "pa0", "pa1", "pa2",
+SEMAPHORES = ["ld0", "ld0b", "ld1", "ld2", "ld3", "ld4", "ld5", "ma0", "ma1", "ma2", "pa0", "pa1", "pa2",
               "sent", "vs", "as1", "qo", "qa", "qg", "cst", "ps", "st"]
+
+
+def _count(mask):
+    return sum((mask >> b) & 1 for b in range(16))
 
 
 def _split(mask, n):
@@ -39,9 +48,13 @@ def rank_program(g, core, T, topo):
     peer = [plane[(k + d) % P] for d in range(1, P)]
     mpeer = [mplane[(km + d) % P] for d in range(1, P)]
     order = [T.rank_of(c) for c in mpeer + [mate] + peer + [core]]
+    ND = len(mpeer)
 
     def sl(t, s, n=1):
         return t[:, s * F:(s + n) * F]
+
+    def home(s):
+        return T.xd[s] if s < ND else sl(T.x, s - ND)
 
     def dst(c):
         rid, pid = topo.addr(c, core)
@@ -54,18 +67,31 @@ def rank_program(g, core, T, topo):
 
     for s, b in enumerate(order):
         q = sy if s % 2 == 0 else a
-        q.dma_start(sl(T.x, s), T.gr[:, b * F:(b + 1) * F]).then_inc(ld[s // 2], 16)
-    v.memset(T.ones[0:12, :], 1.0).then_inc(S.cst, 1)
+        q.dma_start(home(s), T.gr[:, b * F:(b + 1) * F]).then_inc(S.ld0b if s == 1 else ld[s // 2], 16)
+    v.memset(T.w[0:QP, :], 1.0 / (bound * bound)).then_inc(S.cst, 1)
+    v.memset(T.cl[:, 0:QC - 1], 0.0).then_inc(S.cst, 1)
+    v.memset(T.cl[:, QC - 1:QC], 1.0).then_inc(S.cst, 1)
 
     mm = topo.mask(core, mate)
-    ne = len(_split(mm, 1)) and sum((mm >> b) & 1 for b in range(16))
-    rid, pid = topo.addr(mate, core)
+    ne = _count(mm)
+    halves = _split(mm, 2)
     sent = 0
     for p in range(3):
-        g.wait_ge(ld[p], 32)
-        g.remote_dma(out_ap=sl(T.lm, 2 * p, 2), in_ap=sl(T.x, 2 * p, 2), remote_sem=ma[p], local_sem=S.sent,
-                     pid=pid, routing_id=rid, dma_engine_mask=mm)
-        sent += ne
+        trs = []
+        for j, m in enumerate(halves):
+            s = 2 * p + j
+            land = T.lmd[s] if s < ND else T.lm[:]
+            trs.append(RemoteDMATransfer(dst_ids=[dst(mate)], dma_engine_mask=m, remote_sem=ma[p],
+                                         srcs=[home(s)], dsts=[land], alu_op=0))
+            sent += _count(m)
+        if p == 0:
+            g.wait_ge(S.ld0, 16)
+            g.remote_dma_fused(trs[0:1], local_sem=S.sent)
+            g.wait_ge(S.ld0b, 16)
+            g.remote_dma_fused(trs[1:2], local_sem=S.sent)
+        else:
+            g.wait_ge(ld[p], 32)
+            g.remote_dma_fused(trs, local_sem=S.sent)
 
     batches = [[0, 1], [2, 3], [4]]
     for p, ds in enumerate(batches):
@@ -75,14 +101,14 @@ def rank_program(g, core, T, topo):
         trs = []
         for d, m in zip(ds, masks):
             trs.append(RemoteDMATransfer(dst_ids=[dst(peer[d])], dma_engine_mask=m, remote_sem=pa[p],
-                                         srcs=[sl(T.x, 6 + d), sl(T.lm, d)], dsts=[sl(T.lp, d)], alu_op=1))
-            sent += sum((m >> b) & 1 for b in range(16))
+                                         srcs=[home(ND + 1 + d), T.lmd[d]], dsts=[sl(T.lp, d)], alu_op=1))
+            sent += _count(m)
         g.remote_dma_fused(trs, local_sem=S.sent)
 
     acc = T.acc[:, 0:F]
     v.wait_ge(ld[5], 32)
     v.wait_ge(ma[2], ne)
-    v.tensor_tensor(acc, sl(T.x, 11), sl(T.lm, 5), AluOpType.add).then_inc(S.vs, 1)
+    v.tensor_tensor(acc, home(11), T.lm[:], AluOpType.add).then_inc(S.vs, 1)
     n = 1
     for p, ds in enumerate(batches):
         v.wait_ge(pa[p], ne)
@@ -100,7 +126,7 @@ def rank_program(g, core, T, topo):
     common = topo.mask(core, others[0])
     for c in others:
         common &= topo.mask(core, c)
-    ones_m = _split(common, sum((common >> b) & 1 for b in range(16)))
+    ones_m = _split(common, _count(common))
     groups = [others[j::len(ones_m)] for j in range(len(ones_m))]
     trs = []
     for m, grp in zip(ones_m, groups):
@@ -114,24 +140,26 @@ def rank_program(g, core, T, topo):
 
     sy.wait_ge(S.qo, 16)
     sy.wait_ge(S.qa, len(others))
-    sy.dma_start(T.qs[0:12, :], T.qall[:]).then_inc(S.qg, 16)
+    sy.dma_start(T.qs[0:QP, :], T.qall[:]).then_inc(S.qg, 16)
 
-    v.wait_ge(S.qg, 16)
-    v.tensor_reduce(T.sc[0:12, 4:5], T.qs[0:12, :], AxisListType.X, AluOpType.add).then_inc(S.vs, 1)
-    n += 1
-    pe.wait_ge(S.cst, 1)
-    pe.wait_ge(S.vs, n)
-    pe.matmul(T.tot[:, 0:1], T.ones[0:12, :], T.sc[0:12, 4:5], True, True).then_inc(S.ps, 1)
+    pe.wait_ge(S.cst, 3)
+    pe.wait_ge(S.qg, 16)
+    pe.matmul(T.tot[:, 0:QC], T.w[0:QP, :], T.qs[0:QP, :], True, True).then_inc(S.ps, 1)
+    u, ru, su = T.sn[:, QC - 1:QC], T.sc[:, 4:5], T.sc[:, 8:9]
+    v.wait_ge(S.cst, 3)
     v.wait_ge(S.ps, 1)
-    v.tensor_scalar(T.sc[:, 8:9], T.tot[:, 0:1], 1.0 / (bound * bound), 1.0, AluOpType.mult, AluOpType.max).then_inc(S.vs, 1)
+    v.tensor_tensor_scan(T.sn[:], T.tot[:, 0:QC], T.cl[:], 0.0, AluOpType.add, AluOpType.max).then_inc(S.vs, 1)
+    n += 1
+
+    a.wait_ge(S.vs, n)
+    a.activation(su, u, ActivationFunctionType.Sqrt).then_inc(S.as1, 1)
+    v.wait_ge(S.vs, n)
+    v.reciprocal(ru, u).then_inc(S.vs, 1)
     n += 1
     v.wait_ge(S.vs, n)
-    v.reciprocal(T.sc[:, 9:10], T.sc[:, 8:9]).then_inc(S.vs, 1)
+    v.wait_ge(S.as1, 2)
+    v.tensor_scalar(T.yb[:], acc, ru, su, AluOpType.mult, AluOpType.mult).then_inc(S.vs, 1)
     n += 1
-    a.wait_ge(S.vs, n)
-    a.activation(T.sc[:, 10:11], T.sc[:, 9:10], ActivationFunctionType.Sqrt).then_inc(S.as1, 1)
-    a.wait_ge(S.as1, 2)
-    a.activation(T.yb[:], acc, ActivationFunctionType.Copy, scale=T.sc[:, 10:11]).then_inc(S.as1, 1)
-    a.wait_ge(S.as1, 3)
-    a.dma_start(T.y[:], T.yb[:]).then_inc(S.st, 16)
-    a.wait_ge(S.st, 16)
+    sy.wait_ge(S.vs, n)
+    sy.dma_start(T.y[:], T.yb[:]).then_inc(S.st, 16)
+    sy.wait_ge(S.st, 16)

from concourse.bass import DstId, RemoteDMATransfer
from concourse.mybir import AluOpType, AxisListType, ActivationFunctionType

F = 128
QP, QC = 32, 48
SCRATCH = {
    "xd": ("dram", [5, 128, F], "float32"),
    "lmd": ("dram", [5, 128, F], "float32"),
    "x": ("sbuf", [128, 7 * F], "float32"),
    "lm": ("sbuf", [128, F], "float32"),
    "lp": ("sbuf", [128, 5 * F], "float32"),
    "sq": ("sbuf", [128, F], "float32"),
    "yb": ("sbuf", [128, F], "float32"),
    "qs": ("sbuf", [128, QC], "float32"),
    "w": ("sbuf", [128, F], "float32"),
    "cl": ("sbuf", [128, QC], "float32"),
    "sn": ("sbuf", [128, QC], "float32"),
    "sc": ("sbuf", [128, 12], "float32"),
    "qall": ("dram", [12, 128, 1], "float32"),
    "acc": ("psum", [128, 512], "float32"),
    "tot": ("psum", [128, 512], "float32"),
}
SEMAPHORES = ["ld0", "ld0b", "ld1", "ld2", "ld3", "ld4", "ld5", "ma0", "ma1", "ma2", "pa0", "pa1", "pa2",
              "sent", "vs", "as1", "qo", "qa", "qg", "cst", "ps", "st"]


def _count(mask):
    return sum((mask >> b) & 1 for b in range(16))


def _split(mask, n):
    eng = [b for b in range(16) if (mask >> b) & 1]
    per = len(eng) // n
    return [sum(1 << e for e in eng[j * per:(j + 1) * per]) for j in range(n)]


def rank_program(g, core, T, topo):
    me = T.rank_of(core)
    if me is None:
        return
    S = T.sem
    cores = list(T.cores)
    bound = float(T.tables["BOUND"])
    mate = [c for c in cores if topo.mates(core, c)][0]
    plane = [c for c in cores if c == core or topo.same_plane(core, c)]
    mplane = [c for c in cores if c == mate or topo.same_plane(mate, c)]
    k, km, P = plane.index(core), mplane.index(mate), len(plane)
    peer = [plane[(k + d) % P] for d in range(1, P)]
    mpeer = [mplane[(km + d) % P] for d in range(1, P)]
    order = [T.rank_of(c) for c in mpeer + [mate] + peer + [core]]
    ND = len(mpeer)

    def sl(t, s, n=1):
        return t[:, s * F:(s + n) * F]

    def home(s):
        return T.xd[s] if s < ND else sl(T.x, s - ND)

    def dst(c):
        rid, pid = topo.addr(c, core)
        return DstId(rid=rid, pnc=pid)

    v, a, sy, pe = g.vector, g.scalar, g.sync, g.tensor
    ld = [S.ld0, S.ld1, S.ld2, S.ld3, S.ld4, S.ld5]
    ma = [S.ma0, S.ma1, S.ma2]
    pa = [S.pa0, S.pa1, S.pa2]

    for s, b in enumerate(order):
        q = sy if s % 2 == 0 else a
        q.dma_start(home(s), T.gr[:, b * F:(b + 1) * F]).then_inc(S.ld0b if s == 1 else ld[s // 2], 16)
    v.memset(T.w[0:QP, :], 1.0 / (bound * bound)).then_inc(S.cst, 1)
    v.memset(T.cl[:, 0:QC - 1], 0.0).then_inc(S.cst, 1)
    v.memset(T.cl[:, QC - 1:QC], 1.0).then_inc(S.cst, 1)

    mm = topo.mask(core, mate)
    ne = _count(mm)
    halves = _split(mm, 2)
    sent = 0
    for p in range(3):
        trs = []
        for j, m in enumerate(halves):
            s = 2 * p + j
            land = T.lmd[s] if s < ND else T.lm[:]
            trs.append(RemoteDMATransfer(dst_ids=[dst(mate)], dma_engine_mask=m, remote_sem=ma[p],
                                         srcs=[home(s)], dsts=[land], alu_op=0))
            sent += _count(m)
        if p == 0:
            g.wait_ge(S.ld0, 16)
            g.remote_dma_fused(trs[0:1], local_sem=S.sent)
            g.wait_ge(S.ld0b, 16)
            g.remote_dma_fused(trs[1:2], local_sem=S.sent)
        else:
            g.wait_ge(ld[p], 32)
            g.remote_dma_fused(trs, local_sem=S.sent)

    batches = [[0, 1], [2, 3], [4]]
    for p, ds in enumerate(batches):
        g.wait_ge(ld[3 + p], 32)
        g.wait_ge(ma[p], ne)
        masks = _split(topo.mask(core, peer[ds[0]]), len(ds))
        trs = []
        for d, m in zip(ds, masks):
            trs.append(RemoteDMATransfer(dst_ids=[dst(peer[d])], dma_engine_mask=m, remote_sem=pa[p],
                                         srcs=[home(ND + 1 + d), T.lmd[d]], dsts=[sl(T.lp, d)], alu_op=1))
            sent += _count(m)
        g.remote_dma_fused(trs, local_sem=S.sent)

    acc = T.acc[:, 0:F]
    v.wait_ge(ld[5], 32)
    v.wait_ge(ma[2], ne)
    v.tensor_tensor(acc, home(11), T.lm[:], AluOpType.add).then_inc(S.vs, 1)
    n = 1
    for p, ds in enumerate(batches):
        v.wait_ge(pa[p], ne)
        for d in ds:
            v.wait_ge(S.vs, n)
            v.tensor_tensor(acc, acc, sl(T.lp, d), AluOpType.add).then_inc(S.vs, 1)
            n += 1

    a.wait_ge(S.vs, n)
    a.activation(T.sq[:], acc, ActivationFunctionType.Square, accum_out=T.sc[:, 0:1]).then_inc(S.as1, 1)
    a.wait_ge(S.as1, 1)
    a.dma_start(T.qall[me], T.sc[:, 0:1]).then_inc(S.qo, 16)

    others = [c for c in cores if c != core]
    common = topo.mask(core, others[0])
    for c in others:
        common &= topo.mask(core, c)
    ones_m = _split(common, _count(common))
    groups = [others[j::len(ones_m)] for j in range(len(ones_m))]
    trs = []
    for m, grp in zip(ones_m, groups):
        if grp:
            trs.append(RemoteDMATransfer(dst_ids=[dst(c) for c in grp], dma_engine_mask=m, remote_sem=S.qa,
                                         srcs=[T.qall[me]], dsts=[T.qall[me] for c in grp], alu_op=0))
            sent += 1
    g.wait_ge(S.qo, 16)
    g.remote_dma_fused(trs, local_sem=S.sent)
    g.wait_ge(S.sent, sent)

    sy.wait_ge(S.qo, 16)
    sy.wait_ge(S.qa, len(others))
    sy.dma_start(T.qs[0:QP, :], T.qall[:]).then_inc(S.qg, 16)

    pe.wait_ge(S.cst, 3)
    pe.wait_ge(S.qg, 16)
    pe.matmul(T.tot[:, 0:QC], T.w[0:QP, :], T.qs[0:QP, :], True, True).then_inc(S.ps, 1)
    u, ru, su = T.sn[:, QC - 1:QC], T.sc[:, 4:5], T.sc[:, 8:9]
    v.wait_ge(S.cst, 3)
    v.wait_ge(S.ps, 1)
    v.tensor_tensor_scan(T.sn[:], T.tot[:, 0:QC], T.cl[:], 0.0, AluOpType.add, AluOpType.max).then_inc(S.vs, 1)
    n += 1

    a.wait_ge(S.vs, n)
    a.activation(su, u, ActivationFunctionType.Sqrt).then_inc(S.as1, 1)
    v.wait_ge(S.vs, n)
    v.reciprocal(ru, u).then_inc(S.vs, 1)
    n += 1
    v.wait_ge(S.vs, n)
    v.wait_ge(S.as1, 2)
    v.tensor_scalar(T.yb[:], acc, ru, su, AluOpType.mult, AluOpType.mult).then_inc(S.vs, 1)
    n += 1
    sy.wait_ge(S.vs, n)
    sy.dma_start(T.y[:], T.yb[:]).then_inc(S.st, 16)
    sy.wait_ge(S.st, 16)
